import numpy as np, ml_dtypes
CORES = [44,45,46,47,172,173,174,175,300,301,302,303,428,429,430,431]
N = 16
CAP = 256
T = N * CAP
def entries(a): return a.T.reshape(-1)
def pack(v, P): return np.ascontiguousarray(np.asarray(v, np.int32).reshape(-1, P).T)
def lists(rng, how):
    C = rng.integers(0, CAP + 1, (N, N))
    if how == "edge": C = np.array([0, 1, CAP - 1, CAP])[(rng.permutation(N)[:, None] + rng.permutation(N)[None, :]) % 4]
    if how == "full": C[:] = CAP
    if how == "lone": z = int(rng.integers(N)); k = C[z].copy(); C[:] = 0; C[z] = np.maximum(k, 1)
    if how == "none": u, v, w = rng.permutation(N)[:3]; C = np.maximum(C, 1); C[u] = 0; C[:, u] = 0; C[v] = 0; C[:, w] = 0
    if how == "zeros": C = rng.integers(4, CAP, (N, N))
    return {"cnt": np.stack([pack(np.concatenate([c, np.zeros(32 - N, np.int64)]), 16) for c in C])}
def setup_inputs(rng):
    return dict({"x": rng.standard_normal((N, 128, T), dtype=np.float32).astype(ml_dtypes.bfloat16)}, **lists(rng, "uniform"))
def setup_inputs_edge(rng):
    d = setup_inputs(rng); d.update(lists(rng, "edge"))
    for k in ("x",): d[k] = (d[k].astype(np.float32) * 1048576.0).astype(d[k].dtype)
    return d
def setup_inputs_full(rng):
    d = setup_inputs(rng); d.update(lists(rng, "full"))
    for k in ("x",): d[k] = (d[k].astype(np.float32) * (1 / 1024.0)).astype(d[k].dtype)
    return d
def setup_inputs_lone(rng):
    d = setup_inputs(rng); d.update(lists(rng, "lone"))
    return d
def setup_inputs_none(rng):
    d = setup_inputs(rng); d.update(lists(rng, "none"))
    return d
def setup_inputs_zeros(rng):
    d = setup_inputs(rng); d.update(lists(rng, "zeros"))
    K = np.stack([entries(a) for a in d["cnt"]])[:, :N]; B = np.cumsum(K, axis=1) - K
    Z = np.concatenate([B, B + rng.integers(2, K - 1), B + K - 1], axis=1)
    for r in range(N): d["x"][r][:, Z[r]] = 0
    d["x"][:, 0][rng.random((N, T)) < 0.5] = 0
    return d
def check_inputs(x):
    bad = []
    if x["cnt"].min() < 0 or x["cnt"].max() >= CAP + 1: bad.append("cnt out of range")
    if any(entries(a)[N:].any() for a in x["cnt"]): bad.append("an entry from N on isn't 0")
    return bad
def reference(x, cnt):
    C = np.stack([entries(c)[:N] for c in cnt]); S = np.cumsum(C, axis=1) - C
    y = np.zeros((N, 128, T), x.dtype)
    for d in range(N):
        got = np.concatenate([x[r][:, S[r, d]:S[r, d] + C[r, d]] for r in range(N)], axis=1); y[d][:, :got.shape[1]] = got
    return {"y": y}

@@ -1,0 +1,264 @@
+from concourse.bass import DstId, RemoteDMATransfer
+from concourse.mybir import AluOpType, ActivationFunctionType
+
+N, CAP = 16, 256
+W = N * CAP
+SIM_CORES = 512
+
+SCRATCH = {
+    "xs": ("sbuf", [128, W], "bfloat16"),
+    "snd": ("sbuf", [128, W], "bfloat16"),
+    "land": ("sbuf", [128, W + 16], "bfloat16"),
+    "outb": ("sbuf", [128, W], "bfloat16"),
+    "hsb": ("sbuf", [128, 2 * CAP], "bfloat16"),
+    "hdb": ("sbuf", [128, 4 * CAP], "bfloat16"),
+    "call": ("dram", [N, 128, 2], "int32"),
+    "cin": ("sbuf", [16, 2], "int32"),
+    "zi": ("sbuf", [7, 32], "int32"),
+    "ctab": ("sbuf", [16, 32], "int32"),
+    "ones": ("sbuf", [16, 256], "bfloat16"),
+    "six": ("sbuf", [16, 128], "bfloat16"),
+    "qrow": ("sbuf", [16, 128], "bfloat16"),
+    "cidx": ("sbuf", [16, 256], "bfloat16"),
+    "tri": ("sbuf", [16, 256], "bfloat16"),
+    "tri2": ("sbuf", [16, 16], "bfloat16"),
+    "nz": ("sbuf", [128, 1], "float32"),
+    "cf": ("sbuf", [16, 1], "float32"),
+    "lhs": ("sbuf", [16, 128], "bfloat16"),
+    "off": ("sbuf", [128, 256], "uint16"),
+    "offr": ("sbuf", [128, 256], "uint16"),
+    "cb": ("sbuf", [16, 1], "bfloat16"),
+    "dr": ("sbuf", [16, 1], "float32"),
+    "bi": ("sbuf", [16, 1], "int32"),
+    "bl": ("sbuf", [16, 1], "int32"),
+    "blf": ("sbuf", [16, 1], "float32"),
+    "t1": ("sbuf", [16, 1], "float32"),
+    "t2": ("sbuf", [16, 1], "float32"),
+    "rg1": ("sbuf", [16, 256], "bfloat16"),
+    "rg2": ("sbuf", [16, 256], "bfloat16"),
+    "lg1": ("sbuf", [16, 128], "bfloat16"),
+    "lg2": ("sbuf", [16, 128], "bfloat16"),
+    "ps1": ("psum", [128, 512], "float32"),
+    "ps2": ("psum", [128, 512], "float32"),
+    "ps3": ("psum", [128, 512], "float32"),
+}
+SEMAPHORES = ["cl", "zs", "ci", "xl", "cv", "cg", "vs", "lh", "mm1", "ofs", "gD", "gH", "gC", "gS", "gO", "sent",
+              "carr", "arr", "ct", "cbs", "vq", "mb", "rl", "mm2", "ofr", "y0", "y1", "y2", "y3", "stored",
+              "hc", "hs", "hd"]
+
+
+def layout(T, topo):
+    groups, where = [], {}
+    for r in range(N):
+        c = T.cores[r]
+        key = (topo.host(c), topo.chip(c))
+        if key not in where:
+            where[key] = len(groups)
+            groups.append([])
+        groups[where[key]].append(r)
+    helpers, sw, cab, dia = [], [], [], []
+    for ranks in groups:
+        c = T.cores[ranks[0]]
+        helpers.append([k for k in range(SIM_CORES) if topo.host(k) == topo.host(c) and topo.chip(k) == topo.chip(c)
+                        and topo.die(k) != topo.die(c)][:len(ranks)])
+        for b in range(len(groups)):
+            e = T.cores[groups[b][0]]
+            if e == c:
+                continue
+            if topo.rack(topo.host(e)) == topo.rack(topo.host(c)):
+                sw.append(b)
+            elif topo.may_write(c, e):
+                cab.append(b)
+            else:
+                dia.append(b)
+    return groups, helpers, sw, cab, dia
+
+
+def bits(mask):
+    return [1 << k for k in range(16) if (mask >> k) & 1]
+
+
+def parts(mask, n):
+    b = bits(mask)
+    return [sum(b[k:k + n]) for k in range(0, len(b) - n + 1, n)]
+
+
+def rank_program(g, core, T, topo):
+    groups, helpers, sw, cab, dia = layout(T, topo)
+    S = T.sem
+
+    def dst(d):
+        rid, pnc = topo.addr(d, core)
+        return DstId(rid=rid, pnc=pnc)
+
+    def move(to, mask, sem, src, out):
+        return RemoteDMATransfer(dst_ids=[dst(to)], dma_engine_mask=mask, remote_sem=sem, srcs=[src], dsts=[out])
+
+    def blocks(ranks):
+        return slice(CAP * ranks[0], CAP * (ranks[-1] + 1))
+
+    rank = T.rank_of(core)
+    if rank is None:
+        for a in range(len(groups)):
+            if core in helpers[a]:
+                helper(g, T, topo, core, a, helpers[a].index(core), groups, sw, cab, dst, move, blocks)
+        return
+
+    a = [k for k in range(len(groups)) if rank in groups[k]][0]
+    me = groups[a].index(rank)
+    near, cabled, diag = groups[sw[a]], groups[cab[a]], groups[dia[a]]
+    mates_here = [r for r in groups[a] if r != rank]
+    my_helper = helpers[a][me]
+    relay = helpers[sw[a]][me]
+    far = topo.mask(core, T.cores[near[0]])
+    here = topo.mask(core, my_helper) & ~far
+    direct, helped = near[:2], near[2:]
+
+    g.sync.dma_start(T.call[rank, 0:16, :], T.cnt[:]).then_inc(S.cl, 16)
+    g.sync.dma_start(T.xs[:], T.x[:]).then_inc(S.xl, 16)
+    g.scalar.dma_start(T.cin[:], T.cnt[:]).then_inc(S.ci, 16)
+    g.vector.memset(T.zi[:], 0).then_inc(S.zs, 1)
+    g.scalar.wait_ge(S.zs, 1)
+    g.scalar.dma_start(T.call[rank, 16:128, :], T.zi[:]).then_inc(S.cl, 16)
+
+    g.vector.memset(T.ones[:], 1.0).then_inc(S.cv, 1)
+    g.vector.memset(T.six[:], 16.0).then_inc(S.cv, 1)
+    g.vector.memset(T.nz[:], -0.0).then_inc(S.cv, 1)
+    g.vector.memset(T.land[:, W:W + 16], 0.0).then_inc(S.cv, 1)
+    g.iota(T.qrow[:], [[0, 8], [1, 16]], 0, 0, allow_small_or_imprecise_dtypes=True).then_inc(S.cg, 1)
+    g.iota(T.cidx[:], [[1, 256]], 0, 0, allow_small_or_imprecise_dtypes=True).then_inc(S.cg, 1)
+    g.wait_ge(S.cv, 4)
+    g.affine_select(T.tri[:], T.ones[:], [[1, 16], [0, 16]], AluOpType.is_gt, 0.0, 0, -1).then_inc(S.cg, 1)
+    g.affine_select(T.tri2[:], T.ones[:, 0:16], [[1, 16]], AluOpType.is_ge, 0.0, 0, -1).then_inc(S.cg, 1)
+
+    g.wait_ge(S.cl, 32)
+    slot = T.call[rank]
+    outside = [T.cores[r] for r in near + cabled]
+    g.remote_dma_fused([
+        RemoteDMATransfer(dst_ids=[dst(relay)], dma_engine_mask=parts(far, 4)[0], remote_sem=S.hc, srcs=[slot], dsts=[slot]),
+        RemoteDMATransfer(dst_ids=[dst(c) for c in outside], dma_engine_mask=parts(far, 4)[1], remote_sem=S.carr,
+                          srcs=[slot], dsts=[slot] * len(outside)),
+        RemoteDMATransfer(dst_ids=[dst(T.cores[r]) for r in mates_here], dma_engine_mask=here, remote_sem=S.carr,
+                          srcs=[slot], dsts=[slot] * len(mates_here)),
+    ], local_sem=S.sent)
+    n_sent = [16]
+
+    g.vector.wait_ge(S.ci, 16)
+    g.vector.tensor_scalar(T.cf[:], T.cin[:, 0:1], float(-CAP), None, AluOpType.add).then_inc(S.vs, 1)
+    g.vector.wait_ge(S.vs, 1)
+    g.vector.wait_ge(S.cv, 4)
+    g.vector.tensor_scalar(T.lhs[:], T.ones[:, 0:128], T.cf[:, 0:1], None, AluOpType.mult).then_inc(S.lh, 1)
+    t = g.tensor
+    t.wait_ge(S.cv, 4)
+    t.wait_ge(S.cg, 4)
+    for ps in (T.ps1, T.ps2):
+        t.matmul(ps[:, 0:256], T.six[0:1, :], T.cidx[0:1, :], True, False)
+        t.matmul(ps[:, 0:256], T.qrow[0:1, :], T.ones[0:1, :], False, False)
+    t.wait_ge(S.lh, 1)
+    t.matmul(T.ps1[:, 0:256], T.lhs[:], T.tri[:], False, True).then_inc(S.mm1, 1)
+    g.vector.wait_ge(S.mm1, 1)
+    g.vector.tensor_copy(T.off[:], T.ps1[:, 0:256]).then_inc(S.ofs, 1)
+
+    def v_gather(out, win, lst, sem):
+        g.vector.tensor_copy(out, win.indirect(lst)).then_inc(sem, 1)
+
+    def s_gather(out, win, lst, sem):
+        g.scalar.activation(out, win.indirect(lst), ActivationFunctionType.Identity, bias=T.nz[:, 0:1],
+                            scale=1.0).then_inc(sem, 1)
+
+    for q in (g.vector, g.scalar):
+        q.wait_ge(S.ofs, 1)
+        q.wait_ge(S.xl, 16)
+    g.scalar.wait_ge(S.cv, 4)
+    for ranks, sem in ((diag, S.gD), (helped, S.gH), (cabled, S.gC), (direct, S.gS)):
+        h = len(ranks) // 2
+        for rs, gather in ((ranks[:h], v_gather), (ranks[h:], s_gather)):
+            gather(T.snd[:, blocks(rs)], T.xs[:], T.off[:, 16 * rs[0]:16 * (rs[-1] + 1)], sem)
+    for k, r in enumerate(groups[a]):
+        gather = v_gather if k < 2 else s_gather
+        gather((T.land if r == rank else T.snd)[:, blocks([r])], T.xs[:], T.off[:, 16 * r:16 * (r + 1)], S.gO)
+
+    def fused(ranks, masks):
+        g.remote_dma_fused([move(T.cores[r], m, S.arr, T.snd[:, blocks([r])], T.land[:, blocks([rank])])
+                            for r, m in zip(ranks, masks)], local_sem=S.sent)
+        n_sent[0] += sum(len(bits(m)) for r, m in zip(ranks, masks))
+
+    def single(to, mask, sem, ranks, out):
+        rid, pid = topo.addr(to, core)
+        g.remote_dma(out, T.snd[:, blocks(ranks)], sem, S.sent, pid, rid, mask)
+        n_sent[0] += len(bits(mask))
+
+    g.wait_ge(S.gD, 2)
+    single(relay, far, S.hd, diag, T.hdb[:])
+    g.wait_ge(S.gH, 2)
+    single(my_helper, here, S.hs, helped, T.hsb[:])
+    g.wait_ge(S.gC, 2)
+    fused(cabled, parts(far, 2))
+    g.wait_ge(S.gS, 2)
+    fused(direct, parts(far, 4))
+    g.wait_ge(S.gO, 4)
+    fused(mates_here, parts(here, 2))
+
+    g.sync.wait_ge(S.cl, 32)
+    g.sync.wait_ge(S.carr, 8 * 3 + 4 * 8 + 8 * 4)
+    g.sync.dma_start(T.ctab[:], T.call[:, 0:16, :]).then_inc(S.ct, 16)
+    v, A = g.vector, AluOpType
+    got = T.ctab[:, 2 * rank:2 * rank + 1]
+    v.wait_ge(S.ct, 16)
+    v.tensor_copy(T.cb[:], got).then_inc(S.cbs, 1)
+    v.tensor_scalar(T.dr[:], got, -1.0, float(CAP), A.mult, A.add).then_inc(S.vq, 1)
+    t.wait_ge(S.cbs, 1)
+    t.matmul(T.ps3[0:16, 0:1], T.tri2[:], T.cb[:], True, True).then_inc(S.mb, 1)
+    B = T.ps3[0:16, 0:1]
+    v.wait_ge(S.mb, 1)
+    v.tensor_copy(T.bi[:], B).then_inc(S.vq, 1)
+    v.tensor_scalar(T.t1[:], B, -15.0, 1.0 / 16, A.add, A.mult).then_inc(S.vq, 1)
+    v.tensor_scalar(T.t2[:], B, 1.0, 1.0 / 16, A.add, A.mult).then_inc(S.vq, 1)
+    v.wait_ge(S.vq, 4)
+    v.tensor_scalar(T.bl[:], T.bi[:], 15, None, A.bitwise_and).then_inc(S.vq, 1)
+    v.wait_ge(S.cg, 4)
+    v.tensor_scalar(T.rg1[:], T.cidx[:], T.t1[:, 0:1], None, A.is_ge).then_inc(S.rl, 1)
+    v.wait_ge(S.vq, 5)
+    v.tensor_copy(T.blf[:], T.bl[:]).then_inc(S.vq, 1)
+    v.tensor_scalar(T.rg2[:], T.cidx[:], T.t2[:, 0:1], None, A.is_ge).then_inc(S.rl, 1)
+    v.wait_ge(S.vq, 6)
+    v.tensor_scalar(T.lg1[:], T.qrow[:], T.blf[:, 0:1], T.dr[:, 0:1], A.is_ge, A.mult).then_inc(S.rl, 1)
+    v.tensor_scalar(T.lg2[:], T.qrow[:], T.blf[:, 0:1], T.dr[:, 0:1], A.is_lt, A.mult).then_inc(S.rl, 1)
+    t.wait_ge(S.rl, 4)
+    t.matmul(T.ps2[:, 0:256], T.lg1[:], T.rg1[:], False, False)
+    t.matmul(T.ps2[:, 0:256], T.lg2[:], T.rg2[:], False, True).then_inc(S.mm2, 1)
+    v.wait_ge(S.mm2, 1)
+    v.tensor_scalar(T.offr[:], T.ps2[:, 0:256], float(W), None, A.min).then_inc(S.ofr, 1)
+
+    arrivals = 2 * 3 + 2 * 4 + 4 * 4 + 2 * 4
+    for q in (g.vector, g.scalar):
+        q.wait_ge(S.ofr, 1)
+        q.wait_ge(S.gO, 4)
+        q.wait_ge(S.arr, arrivals)
+    ys = [S.y0, S.y1, S.y2, S.y3]
+    for k in range(4):
+        (v_gather if k % 2 == 0 else s_gather)(T.outb[:, 1024 * k:1024 * (k + 1)], T.land[:],
+                                               T.offr[:, 64 * k:64 * (k + 1)], ys[k])
+    for k in range(4):
+        g.sync.wait_ge(ys[k], 1)
+        g.sync.dma_start(T.y[:, 1024 * k:1024 * (k + 1)], T.outb[:, 1024 * k:1024 * (k + 1)]).then_inc(S.stored, 16)
+    g.sync.wait_ge(S.stored, 64)
+    g.wait_ge(S.sent, n_sent[0])
+
+
+def helper(g, T, topo, core, a, i, groups, sw, cab, dst, move, blocks):
+    S = T.sem
+    near, cabled = groups[sw[a]], groups[cab[a]]
+    source, local = near[i], groups[a][i]
+    far = topo.mask(core, T.cores[near[0]])
+    slot = T.call[source]
+    g.wait_ge(S.hc, 4)
+    g.remote_dma_fused([RemoteDMATransfer(dst_ids=[dst(T.cores[r]) for r in cabled], dma_engine_mask=far,
+                                          remote_sem=S.carr, srcs=[slot], dsts=[slot] * len(cabled))], local_sem=S.sent)
+    g.wait_ge(S.hs, 8)
+    g.remote_dma_fused([move(T.cores[r], m, S.arr, T.hsb[:, CAP * k:CAP * (k + 1)], T.land[:, blocks([local])])
+                        for k, (r, m) in enumerate(zip(near[2:], parts(far, 4)))], local_sem=S.sent)
+    g.wait_ge(S.hd, 8)
+    g.remote_dma_fused([move(T.cores[r], m, S.arr, T.hdb[:, CAP * k:CAP * (k + 1)], T.land[:, blocks([source])])
+                        for k, (r, m) in enumerate(zip(cabled, parts(far, 2)))], local_sem=S.sent)
+    g.wait_ge(S.sent, 24)

@@ -4,47 +4,35 @@ from concourse.mybir import AluOpType, ActivationFunctionType
 N, CAP = 16, 256
 W = N * CAP
 SIM_CORES = 512
+PIECES = [1024, 1024, 640, 640, 384, 384]
+
+
+def _sb(rows, cols, dtype):
+    return ("sbuf", [rows, cols], dtype)
+
 
 SCRATCH = {
-    "xs": ("sbuf", [128, W], "bfloat16"),
-    "snd": ("sbuf", [128, W], "bfloat16"),
-    "land": ("sbuf", [128, W + 16], "bfloat16"),
-    "outb": ("sbuf", [128, W], "bfloat16"),
-    "hsb": ("sbuf", [128, 2 * CAP], "bfloat16"),
-    "hdb": ("sbuf", [128, 4 * CAP], "bfloat16"),
+    "xs": _sb(128, W, "bfloat16"),
+    "snd": _sb(128, W, "bfloat16"),
+    "hsn": _sb(128, 4 * CAP, "bfloat16"),
+    "land": _sb(128, W + 16, "bfloat16"),
+    "outb": _sb(128, W, "bfloat16"),
+    "hdb": _sb(128, 4 * CAP, "bfloat16"),
     "call": ("dram", [N, 128, 2], "int32"),
-    "cin": ("sbuf", [16, 2], "int32"),
-    "zi": ("sbuf", [7, 32], "int32"),
-    "ctab": ("sbuf", [16, 32], "int32"),
-    "ones": ("sbuf", [16, 256], "bfloat16"),
-    "six": ("sbuf", [16, 128], "bfloat16"),
-    "qrow": ("sbuf", [16, 128], "bfloat16"),
-    "cidx": ("sbuf", [16, 256], "bfloat16"),
-    "tri": ("sbuf", [16, 256], "bfloat16"),
-    "tri2": ("sbuf", [16, 16], "bfloat16"),
-    "nz": ("sbuf", [128, 1], "float32"),
-    "cf": ("sbuf", [16, 1], "float32"),
-    "lhs": ("sbuf", [16, 128], "bfloat16"),
-    "off": ("sbuf", [128, 256], "uint16"),
-    "offr": ("sbuf", [128, 256], "uint16"),
-    "cb": ("sbuf", [16, 1], "bfloat16"),
-    "dr": ("sbuf", [16, 1], "float32"),
-    "bi": ("sbuf", [16, 1], "int32"),
-    "bl": ("sbuf", [16, 1], "int32"),
-    "blf": ("sbuf", [16, 1], "float32"),
-    "t1": ("sbuf", [16, 1], "float32"),
-    "t2": ("sbuf", [16, 1], "float32"),
-    "rg1": ("sbuf", [16, 256], "bfloat16"),
-    "rg2": ("sbuf", [16, 256], "bfloat16"),
-    "lg1": ("sbuf", [16, 128], "bfloat16"),
-    "lg2": ("sbuf", [16, 128], "bfloat16"),
-    "ps1": ("psum", [128, 512], "float32"),
-    "ps2": ("psum", [128, 512], "float32"),
-    "ps3": ("psum", [128, 512], "float32"),
+    "cin": _sb(16, 2, "int32"), "zi": _sb(7, 32, "int32"), "ctab": _sb(16, 32, "int32"),
+    "ones": _sb(16, 256, "bfloat16"), "six": _sb(16, 128, "bfloat16"), "qrow": _sb(16, 128, "bfloat16"),
+    "cidx": _sb(16, 256, "bfloat16"), "tri": _sb(16, 256, "bfloat16"), "tri2": _sb(16, 16, "bfloat16"),
+    "nz": _sb(128, 1, "float32"), "cf": _sb(16, 1, "float32"), "lhs": _sb(16, 128, "bfloat16"),
+    "off": _sb(128, 256, "uint16"), "offr": _sb(128, 256, "uint16"),
+    "cb": _sb(16, 1, "bfloat16"), "dr": _sb(16, 1, "float32"), "bi": _sb(16, 1, "int32"), "bl": _sb(16, 1, "int32"),
+    "blf": _sb(16, 1, "float32"), "t1": _sb(16, 1, "float32"), "t2": _sb(16, 1, "float32"),
+    "rg1": _sb(16, 256, "bfloat16"), "rg2": _sb(16, 256, "bfloat16"),
+    "lg1": _sb(16, 128, "bfloat16"), "lg2": _sb(16, 128, "bfloat16"),
+    "ps1": ("psum", [128, 512], "float32"), "ps2": ("psum", [128, 512], "float32"), "ps3": ("psum", [128, 512], "float32"),
 }
-SEMAPHORES = ["cl", "zs", "ci", "xl", "cv", "cg", "vs", "lh", "mm1", "ofs", "gD", "gH", "gC", "gS", "gO", "sent",
-              "carr", "arr", "ct", "cbs", "vq", "mb", "rl", "mm2", "ofr", "y0", "y1", "y2", "y3", "stored",
-              "hc", "hs", "hd"]
+SEMAPHORES = ["cl", "zs", "ci", "xl", "cv", "cg", "vs", "lh", "mm1", "ofs", "gD0", "gD1", "gH", "gC", "gO", "sent",
+              "carr", "arr", "ct", "cbs", "vq", "mb", "rl", "mm2", "ofr", "y0", "y1", "y2", "y3", "y4", "y5", "stored",
+              "hc", "hl", "hs", "hd0", "hd1"]
 
 
 def layout(T, topo):
@@ -56,11 +44,15 @@ def layout(T, topo):
             where[key] = len(groups)
             groups.append([])
         groups[where[key]].append(r)
-    helpers, sw, cab, dia = [], [], [], []
+    helpers, porters, carriers, sw, cab, dia = [], [], [], [], [], []
     for ranks in groups:
         c = T.cores[ranks[0]]
-        helpers.append([k for k in range(SIM_CORES) if topo.host(k) == topo.host(c) and topo.chip(k) == topo.chip(c)
-                        and topo.die(k) != topo.die(c)][:len(ranks)])
+        mine = [k for k in range(SIM_CORES) if topo.host(k) == topo.host(c)]
+        helpers.append([k for k in mine if topo.chip(k) == topo.chip(c) and topo.die(k) != topo.die(c)][:len(ranks)])
+        other = [k for k in mine if topo.same_plane(k, c)]
+        other = [k for k in other if topo.chip(k) == topo.chip(other[0])]
+        porters.append(other[0::2])
+        carriers.append(other[1::2])
         for b in range(len(groups)):
             e = T.cores[groups[b][0]]
             if e == c:
@@ -71,7 +63,7 @@ def layout(T, topo):
                 cab.append(b)
             else:
                 dia.append(b)
-    return groups, helpers, sw, cab, dia
+    return groups, helpers, porters, carriers, sw, cab, dia
 
 
 def bits(mask):
@@ -84,7 +76,7 @@ def parts(mask, n):
 
 
 def rank_program(g, core, T, topo):
-    groups, helpers, sw, cab, dia = layout(T, topo)
+    groups, helpers, porters, carriers, sw, cab, dia = layout(T, topo)
     S = T.sem
 
     def dst(d):
@@ -94,25 +86,61 @@ def rank_program(g, core, T, topo):
     def move(to, mask, sem, src, out):
         return RemoteDMATransfer(dst_ids=[dst(to)], dma_engine_mask=mask, remote_sem=sem, srcs=[src], dsts=[out])
 
+    def counts(ranks, source, mask):
+        slot = T.call[source]
+        return RemoteDMATransfer(dst_ids=[dst(T.cores[r]) for r in ranks], dma_engine_mask=mask, remote_sem=S.carr,
+                                 srcs=[slot], dsts=[slot] * len(ranks))
+
     def blocks(ranks):
         return slice(CAP * ranks[0], CAP * (ranks[-1] + 1))
+
+    def onward(source, ks, ranks, masks):
+        g.remote_dma_fused([move(T.cores[r], m, S.arr, T.hdb[:, CAP * k:CAP * (k + 1)], T.land[:, blocks([source])])
+                            for k, r, m in zip(ks, ranks, masks)], local_sem=S.sent)
 
     rank = T.rank_of(core)
     if rank is None:
         for a in range(len(groups)):
+            near, cabled = groups[sw[a]], groups[cab[a]]
+            far = topo.mask(core, T.cores[near[0]]) if core in helpers[a] + porters[a] + carriers[a] else 0
+            f4 = parts(far, 4)
             if core in helpers[a]:
-                helper(g, T, topo, core, a, helpers[a].index(core), groups, sw, cab, dst, move, blocks)
+                source = groups[a][helpers[a].index(core)]
+                g.wait_ge(S.hl, 4)
+                g.remote_dma_fused([counts(cabled, source, far)], local_sem=S.sent)
+                g.wait_ge(S.hs, 8)
+                onward(source, (0, 2, 1, 3), (cabled[2], near[2], cabled[3], near[3]), parts(far, 2))
+                g.wait_ge(S.sent, 16)
+            if core in porters[a]:
+                i = porters[a].index(core)
+                source, to = near[i], carriers[cab[a]][i]
+                slot = T.call[source]
+                g.wait_ge(S.hc, 4)
+                g.remote_dma_fused([move(to, f4[0], S.hc, slot, slot),
+                                    counts([r for r in groups[a] + near if r != source], source, f4[1])], local_sem=S.sent)
+                rid, pid = topo.addr(to, core)
+                for k, sem in enumerate((S.hd0, S.hd1)):
+                    half = T.hdb[:, 2 * CAP * k:2 * CAP * (k + 1)]
+                    g.wait_ge(sem, 8)
+                    g.remote_dma(half, half, sem, S.sent, pid, rid, far)
+                g.wait_ge(S.sent, 24)
+            if core in carriers[a]:
+                source = groups[dia[a]][carriers[a].index(core)]
+                g.wait_ge(S.hc, 4)
+                g.remote_dma_fused([counts(groups[a], source, far)], local_sem=S.sent)
+                for arrived, ks in ((S.hd0, (0, 1)), (S.hd1, (2, 3))):
+                    g.wait_ge(arrived, 8)
+                    onward(source, ks, [groups[a][k] for k in ks], f4)
+                g.wait_ge(S.sent, 24)
         return
 
     a = [k for k in range(len(groups)) if rank in groups[k]][0]
     me = groups[a].index(rank)
     near, cabled, diag = groups[sw[a]], groups[cab[a]], groups[dia[a]]
     mates_here = [r for r in groups[a] if r != rank]
-    my_helper = helpers[a][me]
-    relay = helpers[sw[a]][me]
+    my_helper, porter = helpers[a][me], porters[sw[a]][me]
     far = topo.mask(core, T.cores[near[0]])
     here = topo.mask(core, my_helper) & ~far
-    direct, helped = near[:2], near[2:]
 
     g.sync.dma_start(T.call[rank, 0:16, :], T.cnt[:]).then_inc(S.cl, 16)
     g.sync.dma_start(T.xs[:], T.x[:]).then_inc(S.xl, 16)
@@ -130,18 +158,6 @@ def rank_program(g, core, T, topo):
     g.wait_ge(S.cv, 4)
     g.affine_select(T.tri[:], T.ones[:], [[1, 16], [0, 16]], AluOpType.is_gt, 0.0, 0, -1).then_inc(S.cg, 1)
     g.affine_select(T.tri2[:], T.ones[:, 0:16], [[1, 16]], AluOpType.is_ge, 0.0, 0, -1).then_inc(S.cg, 1)
-
-    g.wait_ge(S.cl, 32)
-    slot = T.call[rank]
-    outside = [T.cores[r] for r in near + cabled]
-    g.remote_dma_fused([
-        RemoteDMATransfer(dst_ids=[dst(relay)], dma_engine_mask=parts(far, 4)[0], remote_sem=S.hc, srcs=[slot], dsts=[slot]),
-        RemoteDMATransfer(dst_ids=[dst(c) for c in outside], dma_engine_mask=parts(far, 4)[1], remote_sem=S.carr,
-                          srcs=[slot], dsts=[slot] * len(outside)),
-        RemoteDMATransfer(dst_ids=[dst(T.cores[r]) for r in mates_here], dma_engine_mask=here, remote_sem=S.carr,
-                          srcs=[slot], dsts=[slot] * len(mates_here)),
-    ], local_sem=S.sent)
-    n_sent = [16]
 
     g.vector.wait_ge(S.ci, 16)
     g.vector.tensor_scalar(T.cf[:], T.cin[:, 0:1], float(-CAP), None, AluOpType.add).then_inc(S.vs, 1)
@@ -170,37 +186,49 @@ def rank_program(g, core, T, topo):
         q.wait_ge(S.ofs, 1)
         q.wait_ge(S.xl, 16)
     g.scalar.wait_ge(S.cv, 4)
-    for ranks, sem in ((diag, S.gD), (helped, S.gH), (cabled, S.gC), (direct, S.gS)):
-        h = len(ranks) // 2
-        for rs, gather in ((ranks[:h], v_gather), (ranks[h:], s_gather)):
-            gather(T.snd[:, blocks(rs)], T.xs[:], T.off[:, 16 * rs[0]:16 * (rs[-1] + 1)], sem)
+
+    def pack(gather, out, ranks, sem):
+        gather(out, T.xs[:], T.off[:, 16 * ranks[0]:16 * (ranks[-1] + 1)], sem)
+
+    for v_ranks, s_ranks, sem in ((diag[:1], diag[1:2], S.gD0), (diag[2:3], diag[3:], S.gD1),
+                                  (cabled[2:], near[2:], S.gH), (cabled[:2], near[:2], S.gC)):
+        for k, (rs, gather) in enumerate(((v_ranks, v_gather), (s_ranks, s_gather))):
+            pack(gather, T.hsn[:, 2 * CAP * k:2 * CAP * (k + 1)] if sem is S.gH else T.snd[:, blocks(rs)], rs, sem)
     for k, r in enumerate(groups[a]):
-        gather = v_gather if k < 2 else s_gather
-        gather((T.land if r == rank else T.snd)[:, blocks([r])], T.xs[:], T.off[:, 16 * r:16 * (r + 1)], S.gO)
+        pack(v_gather if k < 2 else s_gather, (T.land if r == rank else T.snd)[:, blocks([r])], [r], S.gO)
 
-    def fused(ranks, masks):
-        g.remote_dma_fused([move(T.cores[r], m, S.arr, T.snd[:, blocks([r])], T.land[:, blocks([rank])])
-                            for r, m in zip(ranks, masks)], local_sem=S.sent)
-        n_sent[0] += sum(len(bits(m)) for r, m in zip(ranks, masks))
+    n_sent = [0]
 
-    def single(to, mask, sem, ranks, out):
+    def fused(transfers, engines):
+        g.remote_dma_fused(transfers, local_sem=S.sent)
+        n_sent[0] += engines
+
+    def deliver(ranks, masks):
+        fused([move(T.cores[r], m, S.arr, T.snd[:, blocks([r])], T.land[:, blocks([rank])]) for r, m in zip(ranks, masks)],
+              sum(len(bits(m)) for r, m in zip(ranks, masks)))
+
+    def single(to, mask, sem, src, out):
         rid, pid = topo.addr(to, core)
-        g.remote_dma(out, T.snd[:, blocks(ranks)], sem, S.sent, pid, rid, mask)
+        g.remote_dma(out, src, sem, S.sent, pid, rid, mask)
         n_sent[0] += len(bits(mask))
 
-    g.wait_ge(S.gD, 2)
-    single(relay, far, S.hd, diag, T.hdb[:])
+    slot = T.call[rank]
+    f4 = parts(far, 4)
+    g.wait_ge(S.cl, 32)
+    fused([move(my_helper, f4[0], S.hl, slot, slot), move(porter, f4[1], S.hc, slot, slot)], 8)
+    g.wait_ge(S.gD0, 2)
+    single(porter, far, S.hd0, T.snd[:, blocks(diag[:2])], T.hdb[:, 0:2 * CAP])
+    g.wait_ge(S.gD1, 2)
+    single(porter, far, S.hd1, T.snd[:, blocks(diag[2:])], T.hdb[:, 2 * CAP:4 * CAP])
     g.wait_ge(S.gH, 2)
-    single(my_helper, here, S.hs, helped, T.hsb[:])
+    single(my_helper, here, S.hs, T.hsn[:], T.hdb[:])
     g.wait_ge(S.gC, 2)
-    fused(cabled, parts(far, 2))
-    g.wait_ge(S.gS, 2)
-    fused(direct, parts(far, 4))
+    deliver([cabled[0], near[0], cabled[1], near[1]], parts(far, 2))
     g.wait_ge(S.gO, 4)
-    fused(mates_here, parts(here, 2))
+    deliver(mates_here, parts(here, 2))
 
     g.sync.wait_ge(S.cl, 32)
-    g.sync.wait_ge(S.carr, 8 * 3 + 4 * 8 + 8 * 4)
+    g.sync.wait_ge(S.carr, 4 * 3 + 4 * 4 + 8 * 4 + 8 * 4)
     g.sync.dma_start(T.ctab[:], T.call[:, 0:16, :]).then_inc(S.ct, 16)
     v, A = g.vector, AluOpType
     got = T.ctab[:, 2 * rank:2 * rank + 1]
@@ -230,35 +258,17 @@ def rank_program(g, core, T, topo):
     v.wait_ge(S.mm2, 1)
     v.tensor_scalar(T.offr[:], T.ps2[:, 0:256], float(W), None, A.min).then_inc(S.ofr, 1)
 
-    arrivals = 2 * 3 + 2 * 4 + 4 * 4 + 2 * 4
+    arrivals = 2 * 3 + 2 * 8 + 4 * 4
     for q in (g.vector, g.scalar):
         q.wait_ge(S.ofr, 1)
         q.wait_ge(S.gO, 4)
         q.wait_ge(S.arr, arrivals)
-    ys = [S.y0, S.y1, S.y2, S.y3]
-    for k in range(4):
-        (v_gather if k % 2 == 0 else s_gather)(T.outb[:, 1024 * k:1024 * (k + 1)], T.land[:],
-                                               T.offr[:, 64 * k:64 * (k + 1)], ys[k])
-    for k in range(4):
-        g.sync.wait_ge(ys[k], 1)
-        g.sync.dma_start(T.y[:, 1024 * k:1024 * (k + 1)], T.outb[:, 1024 * k:1024 * (k + 1)]).then_inc(S.stored, 16)
-    g.sync.wait_ge(S.stored, 64)
+    p = 0
+    for k, w in enumerate(PIECES):
+        ready = S["y%d" % k]
+        (v_gather if k % 2 == 0 else s_gather)(T.outb[:, p:p + w], T.land[:], T.offr[:, p // 16:(p + w) // 16], ready)
+        g.sync.wait_ge(ready, 1)
+        g.sync.dma_start(T.y[:, p:p + w], T.outb[:, p:p + w]).then_inc(S.stored, 16)
+        p += w
+    g.sync.wait_ge(S.stored, 16 * len(PIECES))
     g.wait_ge(S.sent, n_sent[0])
-
-
-def helper(g, T, topo, core, a, i, groups, sw, cab, dst, move, blocks):
-    S = T.sem
-    near, cabled = groups[sw[a]], groups[cab[a]]
-    source, local = near[i], groups[a][i]
-    far = topo.mask(core, T.cores[near[0]])
-    slot = T.call[source]
-    g.wait_ge(S.hc, 4)
-    g.remote_dma_fused([RemoteDMATransfer(dst_ids=[dst(T.cores[r]) for r in cabled], dma_engine_mask=far,
-                                          remote_sem=S.carr, srcs=[slot], dsts=[slot] * len(cabled))], local_sem=S.sent)
-    g.wait_ge(S.hs, 8)
-    g.remote_dma_fused([move(T.cores[r], m, S.arr, T.hsb[:, CAP * k:CAP * (k + 1)], T.land[:, blocks([local])])
-                        for k, (r, m) in enumerate(zip(near[2:], parts(far, 4)))], local_sem=S.sent)
-    g.wait_ge(S.hd, 8)
-    g.remote_dma_fused([move(T.cores[r], m, S.arr, T.hdb[:, CAP * k:CAP * (k + 1)], T.land[:, blocks([source])])
-                        for k, (r, m) in enumerate(zip(cabled, parts(far, 2)))], local_sem=S.sent)
-    g.wait_ge(S.sent, 24)

@@ -3,8 +3,9 @@ from concourse.mybir import AluOpType, ActivationFunctionType
 
 N, CAP = 16, 256
 W = N * CAP
+HALF = W // 2
 SIM_CORES = 512
-PIECES = [1024, 1024, 640, 640, 384, 384]
+PIECES = [512, 512, 640, 640, 512, 512, 384, 384]
 
 
 def _sb(rows, cols, dtype):
@@ -14,10 +15,11 @@ def _sb(rows, cols, dtype):
 SCRATCH = {
     "xs": _sb(128, W, "bfloat16"),
     "snd": _sb(128, W, "bfloat16"),
-    "hsn": _sb(128, 4 * CAP, "bfloat16"),
+    "hsn": _sb(128, 6 * CAP, "bfloat16"),
     "land": _sb(128, W + 16, "bfloat16"),
     "outb": _sb(128, W, "bfloat16"),
-    "hdb": _sb(128, 4 * CAP, "bfloat16"),
+    "hdb": _sb(128, 6 * CAP, "bfloat16"),
+    "dd": ("dram", [128, CAP], "bfloat16"),
     "call": ("dram", [N, 128, 2], "int32"),
     "cin": _sb(16, 2, "int32"), "zi": _sb(7, 32, "int32"), "ctab": _sb(16, 32, "int32"),
     "ones": _sb(16, 256, "bfloat16"), "six": _sb(16, 128, "bfloat16"), "qrow": _sb(16, 128, "bfloat16"),
@@ -30,9 +32,9 @@ SCRATCH = {
     "lg1": _sb(16, 128, "bfloat16"), "lg2": _sb(16, 128, "bfloat16"),
     "ps1": ("psum", [128, 512], "float32"), "ps2": ("psum", [128, 512], "float32"), "ps3": ("psum", [128, 512], "float32"),
 }
-SEMAPHORES = ["cl", "zs", "ci", "xl", "cv", "cg", "vs", "lh", "mm1", "ofs", "gD0", "gD1", "gH", "gC", "gO", "sent",
-              "carr", "arr", "ct", "cbs", "vq", "mb", "rl", "mm2", "ofr", "y0", "y1", "y2", "y3", "y4", "y5", "stored",
-              "hc", "hl", "hs", "hd0", "hd1"]
+SEMAPHORES = ["cl", "zs", "ci", "xl0", "xl1", "cv", "cg", "vs", "lh", "mm1", "ofs", "gN", "gD0", "gD1", "gH", "gC", "gO", "sent",
+              "carr", "arr", "ct", "cbs", "vq", "mb", "rl", "mm2", "ofr", "stored", "hc", "hl", "hn", "hs", "hd"]
+SEMAPHORES += ["y%d" % k for k in range(len(PIECES))]
 
 
 def layout(T, topo):
@@ -49,10 +51,11 @@ def layout(T, topo):
         c = T.cores[ranks[0]]
         mine = [k for k in range(SIM_CORES) if topo.host(k) == topo.host(c)]
         helpers.append([k for k in mine if topo.chip(k) == topo.chip(c) and topo.die(k) != topo.die(c)][:len(ranks)])
-        other = [k for k in mine if topo.same_plane(k, c)]
-        other = [k for k in other if topo.chip(k) == topo.chip(other[0])]
-        porters.append(other[0::2])
-        carriers.append(other[1::2])
+        plane = [k for k in mine if topo.same_plane(k, c)]
+        same = [k for k in plane if topo.die(k) == topo.die(c)][:2 * N]
+        pool = [k for k in plane if topo.die(k) != topo.die(c)][:2 * N - len(same)] + same
+        porters.append(pool[0::2])
+        carriers.append(pool[1::2])
         for b in range(len(groups)):
             e = T.cores[groups[b][0]]
             if e == c:
@@ -64,6 +67,10 @@ def layout(T, topo):
             else:
                 dia.append(b)
     return groups, helpers, porters, carriers, sw, cab, dia
+
+
+def early(ranks):
+    return CAP * (ranks[-1] + 1) <= HALF
 
 
 def bits(mask):
@@ -94,9 +101,12 @@ def rank_program(g, core, T, topo):
     def blocks(ranks):
         return slice(CAP * ranks[0], CAP * (ranks[-1] + 1))
 
-    def onward(source, ks, ranks, masks):
-        g.remote_dma_fused([move(T.cores[r], m, S.arr, T.hdb[:, CAP * k:CAP * (k + 1)], T.land[:, blocks([source])])
-                            for k, r, m in zip(ks, ranks, masks)], local_sem=S.sent)
+    def piece(t, k, n):
+        return t[:, CAP * k:CAP * (k + n)]
+
+    def onward(source, k0, ranks, masks):
+        g.remote_dma_fused([move(T.cores[r], m, S.arr, piece(T.hdb, k0 + k, 1), T.land[:, blocks([source])])
+                            for k, (r, m) in enumerate(zip(ranks, masks))], local_sem=S.sent)
 
     rank = T.rank_of(core)
     if rank is None:
@@ -108,46 +118,52 @@ def rank_program(g, core, T, topo):
                 source = groups[a][helpers[a].index(core)]
                 g.wait_ge(S.hl, 4)
                 g.remote_dma_fused([counts(cabled, source, far)], local_sem=S.sent)
-                g.wait_ge(S.hs, 8)
-                onward(source, (0, 2, 1, 3), (cabled[2], near[2], cabled[3], near[3]), parts(far, 2))
-                g.wait_ge(S.sent, 16)
+                for which in ("near", "cabled") if early(near) else ("cabled", "near"):
+                    if which == "near":
+                        g.wait_ge(S.hn, 8)
+                        onward(source, 0, near, parts(far, 2))
+                    else:
+                        g.wait_ge(S.hs, 8)
+                        onward(source, 4, cabled[2:], f4)
+                g.wait_ge(S.sent, 24)
             if core in porters[a]:
                 i = porters[a].index(core)
-                source, to = near[i], carriers[cab[a]][i]
+                k, source, to = i // 4, groups[a][i % 4], carriers[cab[a]][i]
+                others = [r for r in groups[a] + near if r != source]
                 slot = T.call[source]
                 g.wait_ge(S.hc, 4)
                 g.remote_dma_fused([move(to, f4[0], S.hc, slot, slot),
-                                    counts([r for r in groups[a] + near if r != source], source, f4[1])], local_sem=S.sent)
+                                    counts(others[2 * k:2 * k + 2], source, f4[1])], local_sem=S.sent)
                 rid, pid = topo.addr(to, core)
-                for k, sem in enumerate((S.hd0, S.hd1)):
-                    half = T.hdb[:, 2 * CAP * k:2 * CAP * (k + 1)]
-                    g.wait_ge(sem, 8)
-                    g.remote_dma(half, half, sem, S.sent, pid, rid, far)
-                g.wait_ge(S.sent, 24)
+                g.wait_ge(S.hd, 4)
+                g.remote_dma(T.dd[:], T.dd[:], S.hd, S.sent, pid, rid, far)
+                g.wait_ge(S.sent, 16)
             if core in carriers[a]:
-                source = groups[dia[a]][carriers[a].index(core)]
+                i = carriers[a].index(core)
+                source, to = cabled[i % 4], near[i // 4]
                 g.wait_ge(S.hc, 4)
-                g.remote_dma_fused([counts(groups[a], source, far)], local_sem=S.sent)
-                for arrived, ks in ((S.hd0, (0, 1)), (S.hd1, (2, 3))):
-                    g.wait_ge(arrived, 8)
-                    onward(source, ks, [groups[a][k] for k in ks], f4)
-                g.wait_ge(S.sent, 24)
+                g.remote_dma_fused([counts([to], source, far)], local_sem=S.sent)
+                rid, pid = topo.addr(T.cores[to], core)
+                g.wait_ge(S.hd, 8)
+                g.remote_dma(T.land[:, blocks([source])], T.dd[:], S.arr, S.sent, pid, rid, far)
+                g.wait_ge(S.sent, 16)
         return
 
     a = [k for k in range(len(groups)) if rank in groups[k]][0]
     me = groups[a].index(rank)
     near, cabled, diag = groups[sw[a]], groups[cab[a]], groups[dia[a]]
     mates_here = [r for r in groups[a] if r != rank]
-    my_helper, porter = helpers[a][me], porters[sw[a]][me]
+    my_helper, my_porters = helpers[a][me], porters[a][me::4]
     far = topo.mask(core, T.cores[near[0]])
     here = topo.mask(core, my_helper) & ~far
 
-    g.sync.dma_start(T.call[rank, 0:16, :], T.cnt[:]).then_inc(S.cl, 16)
-    g.sync.dma_start(T.xs[:], T.x[:]).then_inc(S.xl, 16)
-    g.scalar.dma_start(T.cin[:], T.cnt[:]).then_inc(S.ci, 16)
     g.vector.memset(T.zi[:], 0).then_inc(S.zs, 1)
-    g.scalar.wait_ge(S.zs, 1)
-    g.scalar.dma_start(T.call[rank, 16:128, :], T.zi[:]).then_inc(S.cl, 16)
+    g.scalar.dma_start(T.cin[:], T.cnt[:]).then_inc(S.ci, 16)
+    g.sync.dma_start(T.call[rank, 0:16, :], T.cnt[:]).then_inc(S.cl, 16)
+    g.sync.wait_ge(S.zs, 1)
+    g.sync.dma_start(T.call[rank, 16:128, :], T.zi[:]).then_inc(S.cl, 16)
+    g.sync.dma_start(T.xs[:, :HALF], T.x[:, :HALF]).then_inc(S.xl0, 16)
+    g.sync.dma_start(T.xs[:, HALF:], T.x[:, HALF:]).then_inc(S.xl1, 16)
 
     g.vector.memset(T.ones[:], 1.0).then_inc(S.cv, 1)
     g.vector.memset(T.six[:], 16.0).then_inc(S.cv, 1)
@@ -182,20 +198,30 @@ def rank_program(g, core, T, topo):
         g.scalar.activation(out, win.indirect(lst), ActivationFunctionType.Identity, bias=T.nz[:, 0:1],
                             scale=1.0).then_inc(sem, 1)
 
+    def pack(gather, out, ranks, sem, soon):
+        gather(out, T.xs[:, :HALF] if soon else T.xs[:], T.off[:, 16 * ranks[0]:16 * (ranks[-1] + 1)], sem)
+
+    plan = [("D0", diag[:2], piece(T.snd, diag[0], 1), piece(T.snd, diag[1], 1)),
+            ("D1", diag[2:], piece(T.snd, diag[2], 1), piece(T.snd, diag[3], 1)),
+            ("N", near, piece(T.hsn, 0, 2), piece(T.hsn, 2, 2)),
+            ("H", cabled[2:], piece(T.hsn, 4, 1), piece(T.hsn, 5, 1)),
+            ("C", cabled[:2], piece(T.snd, cabled[0], 1), piece(T.snd, cabled[1], 1))]
+    soon = [e for e in plan if early(e[1])]
+    late = [e for e in plan if not early(e[1])]
     for q in (g.vector, g.scalar):
         q.wait_ge(S.ofs, 1)
-        q.wait_ge(S.xl, 16)
+        q.wait_ge(S.xl0, 16)
     g.scalar.wait_ge(S.cv, 4)
-
-    def pack(gather, out, ranks, sem):
-        gather(out, T.xs[:], T.off[:, 16 * ranks[0]:16 * (ranks[-1] + 1)], sem)
-
-    for v_ranks, s_ranks, sem in ((diag[:1], diag[1:2], S.gD0), (diag[2:3], diag[3:], S.gD1),
-                                  (cabled[2:], near[2:], S.gH), (cabled[:2], near[:2], S.gC)):
-        for k, (rs, gather) in enumerate(((v_ranks, v_gather), (s_ranks, s_gather))):
-            pack(gather, T.hsn[:, 2 * CAP * k:2 * CAP * (k + 1)] if sem is S.gH else T.snd[:, blocks(rs)], rs, sem)
+    for entries, first in ((soon, True), (late, False)):
+        if not first:
+            g.vector.wait_ge(S.xl1, 16)
+            g.scalar.wait_ge(S.xl1, 16)
+        for name, ranks, v_out, s_out in entries:
+            n = len(ranks) // 2
+            pack(v_gather, v_out, ranks[:n], S["g" + name], first)
+            pack(s_gather, s_out, ranks[n:], S["g" + name], first)
     for k, r in enumerate(groups[a]):
-        pack(v_gather if k < 2 else s_gather, (T.land if r == rank else T.snd)[:, blocks([r])], [r], S.gO)
+        pack(v_gather if k < 2 else s_gather, (T.land if r == rank else T.snd)[:, blocks([r])], [r], S.gO, early([r]))
 
     n_sent = [0]
 
@@ -207,25 +233,36 @@ def rank_program(g, core, T, topo):
         fused([move(T.cores[r], m, S.arr, T.snd[:, blocks([r])], T.land[:, blocks([rank])]) for r, m in zip(ranks, masks)],
               sum(len(bits(m)) for r, m in zip(ranks, masks)))
 
-    def single(to, mask, sem, src, out):
-        rid, pid = topo.addr(to, core)
-        g.remote_dma(out, src, sem, S.sent, pid, rid, mask)
-        n_sent[0] += len(bits(mask))
+    def to_helper(sem, k, n):
+        rid, pid = topo.addr(my_helper, core)
+        g.remote_dma(piece(T.hdb, k, n), piece(T.hsn, k, n), sem, S.sent, pid, rid, here)
+        n_sent[0] += len(bits(here))
+
+    def to_porters(ks):
+        fused([move(my_porters[k], m, S.hd, T.snd[:, blocks([diag[k]])], T.dd[:]) for k, m in zip(ks, f4)], 8)
 
     slot = T.call[rank]
     f4 = parts(far, 4)
     g.wait_ge(S.cl, 32)
-    fused([move(my_helper, f4[0], S.hl, slot, slot), move(porter, f4[1], S.hc, slot, slot)], 8)
-    g.wait_ge(S.gD0, 2)
-    single(porter, far, S.hd0, T.snd[:, blocks(diag[:2])], T.hdb[:, 0:2 * CAP])
-    g.wait_ge(S.gD1, 2)
-    single(porter, far, S.hd1, T.snd[:, blocks(diag[2:])], T.hdb[:, 2 * CAP:4 * CAP])
-    g.wait_ge(S.gH, 2)
-    single(my_helper, here, S.hs, T.hsn[:], T.hdb[:])
-    g.wait_ge(S.gC, 2)
-    deliver([cabled[0], near[0], cabled[1], near[1]], parts(far, 2))
+    fused([move(my_helper, f4[0], S.hl, slot, slot),
+           RemoteDMATransfer(dst_ids=[dst(p) for p in my_porters], dma_engine_mask=f4[1], remote_sem=S.hc, srcs=[slot],
+                             dsts=[slot] * len(my_porters))], 8)
+    for entry in soon + late:
+        name = entry[0]
+        g.wait_ge(S["g" + name], 2)
+        if name == "D0":
+            to_porters((0, 1))
+        elif name == "D1":
+            to_porters((2, 3))
+        elif name == "N":
+            to_helper(S.hn, 0, 4)
+        elif name == "H":
+            to_helper(S.hs, 4, 2)
+        else:
+            deliver(cabled[:2], f4)
     g.wait_ge(S.gO, 4)
-    deliver(mates_here, parts(here, 2))
+    deliver(mates_here[:2], parts(here, 4))
+    deliver(mates_here[2:], [here])
 
     g.sync.wait_ge(S.cl, 32)
     g.sync.wait_ge(S.carr, 4 * 3 + 4 * 4 + 8 * 4 + 8 * 4)
@@ -258,7 +295,9 @@ def rank_program(g, core, T, topo):
     v.wait_ge(S.mm2, 1)
     v.tensor_scalar(T.offr[:], T.ps2[:, 0:256], float(W), None, A.min).then_inc(S.ofr, 1)
 
-    arrivals = 2 * 3 + 2 * 8 + 4 * 4
+    arrivals = 2 * 4 + 4 * 4 + 8 * 4
+    for r in mates_here:
+        arrivals += 8 if [q for q in groups[a] if q != r][-1] == rank else 4
     for q in (g.vector, g.scalar):
         q.wait_ge(S.ofr, 1)
         q.wait_ge(S.gO, 4)

from concourse.bass import DstId, RemoteDMATransfer
from concourse.mybir import AluOpType, ActivationFunctionType

N, CAP = 16, 256
W = N * CAP
HALF = W // 2
SIM_CORES = 512
PIECES = [512, 512, 640, 640, 512, 512, 384, 384]


def _sb(rows, cols, dtype):
    return ("sbuf", [rows, cols], dtype)


SCRATCH = {
    "xs": _sb(128, W, "bfloat16"),
    "snd": _sb(128, W, "bfloat16"),
    "hsn": _sb(128, 6 * CAP, "bfloat16"),
    "land": _sb(128, W + 16, "bfloat16"),
    "outb": _sb(128, W, "bfloat16"),
    "hdb": _sb(128, 6 * CAP, "bfloat16"),
    "dd": ("dram", [128, CAP], "bfloat16"),
    "call": ("dram", [N, 128, 2], "int32"),
    "cin": _sb(16, 2, "int32"), "zi": _sb(7, 32, "int32"), "ctab": _sb(16, 32, "int32"),
    "ones": _sb(16, 256, "bfloat16"), "six": _sb(16, 128, "bfloat16"), "qrow": _sb(16, 128, "bfloat16"),
    "cidx": _sb(16, 256, "bfloat16"), "tri": _sb(16, 256, "bfloat16"), "tri2": _sb(16, 16, "bfloat16"),
    "nz": _sb(128, 1, "float32"), "cf": _sb(16, 1, "float32"), "lhs": _sb(16, 128, "bfloat16"),
    "off": _sb(128, 256, "uint16"), "offr": _sb(128, 256, "uint16"),
    "cb": _sb(16, 1, "bfloat16"), "dr": _sb(16, 1, "float32"), "bi": _sb(16, 1, "int32"), "bl": _sb(16, 1, "int32"),
    "blf": _sb(16, 1, "float32"), "t1": _sb(16, 1, "float32"), "t2": _sb(16, 1, "float32"),
    "rg1": _sb(16, 256, "bfloat16"), "rg2": _sb(16, 256, "bfloat16"),
    "lg1": _sb(16, 128, "bfloat16"), "lg2": _sb(16, 128, "bfloat16"),
    "ps1": ("psum", [128, 512], "float32"), "ps2": ("psum", [128, 512], "float32"), "ps3": ("psum", [128, 512], "float32"),
}
SEMAPHORES = ["cl", "zs", "ci", "xl0", "xl1", "cv", "cg", "vs", "lh", "mm1", "ofs", "gN", "gD0", "gD1", "gH", "gC", "gO", "sent",
              "carr", "arr", "ct", "cbs", "vq", "mb", "rl", "mm2", "ofr", "stored", "hc", "hl", "hn", "hs", "hd"]
SEMAPHORES += ["y%d" % k for k in range(len(PIECES))]


def layout(T, topo):
    groups, where = [], {}
    for r in range(N):
        c = T.cores[r]
        key = (topo.host(c), topo.chip(c))
        if key not in where:
            where[key] = len(groups)
            groups.append([])
        groups[where[key]].append(r)
    helpers, porters, carriers, sw, cab, dia = [], [], [], [], [], []
    for ranks in groups:
        c = T.cores[ranks[0]]
        mine = [k for k in range(SIM_CORES) if topo.host(k) == topo.host(c)]
        helpers.append([k for k in mine if topo.chip(k) == topo.chip(c) and topo.die(k) != topo.die(c)][:len(ranks)])
        plane = [k for k in mine if topo.same_plane(k, c)]
        same = [k for k in plane if topo.die(k) == topo.die(c)][:2 * N]
        pool = [k for k in plane if topo.die(k) != topo.die(c)][:2 * N - len(same)] + same
        porters.append(pool[0::2])
        carriers.append(pool[1::2])
        for b in range(len(groups)):
            e = T.cores[groups[b][0]]
            if e == c:
                continue
            if topo.rack(topo.host(e)) == topo.rack(topo.host(c)):
                sw.append(b)
            elif topo.may_write(c, e):
                cab.append(b)
            else:
                dia.append(b)
    return groups, helpers, porters, carriers, sw, cab, dia


def early(ranks):
    return CAP * (ranks[-1] + 1) <= HALF


def bits(mask):
    return [1 << k for k in range(16) if (mask >> k) & 1]


def parts(mask, n):
    b = bits(mask)
    return [sum(b[k:k + n]) for k in range(0, len(b) - n + 1, n)]


def rank_program(g, core, T, topo):
    groups, helpers, porters, carriers, sw, cab, dia = layout(T, topo)
    S = T.sem

    def dst(d):
        rid, pnc = topo.addr(d, core)
        return DstId(rid=rid, pnc=pnc)

    def move(to, mask, sem, src, out):
        return RemoteDMATransfer(dst_ids=[dst(to)], dma_engine_mask=mask, remote_sem=sem, srcs=[src], dsts=[out])

    def counts(ranks, source, mask):
        slot = T.call[source]
        return RemoteDMATransfer(dst_ids=[dst(T.cores[r]) for r in ranks], dma_engine_mask=mask, remote_sem=S.carr,
                                 srcs=[slot], dsts=[slot] * len(ranks))

    def blocks(ranks):
        return slice(CAP * ranks[0], CAP * (ranks[-1] + 1))

    def piece(t, k, n):
        return t[:, CAP * k:CAP * (k + n)]

    def onward(source, k0, ranks, masks):
        g.remote_dma_fused([move(T.cores[r], m, S.arr, piece(T.hdb, k0 + k, 1), T.land[:, blocks([source])])
                            for k, (r, m) in enumerate(zip(ranks, masks))], local_sem=S.sent)

    rank = T.rank_of(core)
    if rank is None:
        for a in range(len(groups)):
            near, cabled = groups[sw[a]], groups[cab[a]]
            far = topo.mask(core, T.cores[near[0]]) if core in helpers[a] + porters[a] + carriers[a] else 0
            f4 = parts(far, 4)
            if core in helpers[a]:
                source = groups[a][helpers[a].index(core)]
                g.wait_ge(S.hl, 4)
                g.remote_dma_fused([counts(cabled, source, far)], local_sem=S.sent)
                for which in ("near", "cabled") if early(near) else ("cabled", "near"):
                    if which == "near":
                        g.wait_ge(S.hn, 8)
                        onward(source, 0, near, parts(far, 2))
                    else:
                        g.wait_ge(S.hs, 8)
                        onward(source, 4, cabled[2:], f4)
                g.wait_ge(S.sent, 24)
            if core in porters[a]:
                i = porters[a].index(core)
                k, source, to = i // 4, groups[a][i % 4], carriers[cab[a]][i]
                others = [r for r in groups[a] + near if r != source]
                slot = T.call[source]
                g.wait_ge(S.hc, 4)
                g.remote_dma_fused([move(to, f4[0], S.hc, slot, slot),
                                    counts(others[2 * k:2 * k + 2], source, f4[1])], local_sem=S.sent)
                rid, pid = topo.addr(to, core)
                g.wait_ge(S.hd, 4)
                g.remote_dma(T.dd[:], T.dd[:], S.hd, S.sent, pid, rid, far)
                g.wait_ge(S.sent, 16)
            if core in carriers[a]:
                i = carriers[a].index(core)
                source, to = cabled[i % 4], near[i // 4]
                g.wait_ge(S.hc, 4)
                g.remote_dma_fused([counts([to], source, far)], local_sem=S.sent)
                rid, pid = topo.addr(T.cores[to], core)
                g.wait_ge(S.hd, 8)
                g.remote_dma(T.land[:, blocks([source])], T.dd[:], S.arr, S.sent, pid, rid, far)
                g.wait_ge(S.sent, 16)
        return

    a = [k for k in range(len(groups)) if rank in groups[k]][0]
    me = groups[a].index(rank)
    near, cabled, diag = groups[sw[a]], groups[cab[a]], groups[dia[a]]
    mates_here = [r for r in groups[a] if r != rank]
    my_helper, my_porters = helpers[a][me], porters[a][me::4]
    far = topo.mask(core, T.cores[near[0]])
    here = topo.mask(core, my_helper) & ~far

    g.vector.memset(T.zi[:], 0).then_inc(S.zs, 1)
    g.scalar.dma_start(T.cin[:], T.cnt[:]).then_inc(S.ci, 16)
    g.sync.dma_start(T.call[rank, 0:16, :], T.cnt[:]).then_inc(S.cl, 16)
    g.sync.wait_ge(S.zs, 1)
    g.sync.dma_start(T.call[rank, 16:128, :], T.zi[:]).then_inc(S.cl, 16)
    g.sync.dma_start(T.xs[:, :HALF], T.x[:, :HALF]).then_inc(S.xl0, 16)
    g.sync.dma_start(T.xs[:, HALF:], T.x[:, HALF:]).then_inc(S.xl1, 16)

    g.vector.memset(T.ones[:], 1.0).then_inc(S.cv, 1)
    g.vector.memset(T.six[:], 16.0).then_inc(S.cv, 1)
    g.vector.memset(T.nz[:], -0.0).then_inc(S.cv, 1)
    g.vector.memset(T.land[:, W:W + 16], 0.0).then_inc(S.cv, 1)
    g.iota(T.qrow[:], [[0, 8], [1, 16]], 0, 0, allow_small_or_imprecise_dtypes=True).then_inc(S.cg, 1)
    g.iota(T.cidx[:], [[1, 256]], 0, 0, allow_small_or_imprecise_dtypes=True).then_inc(S.cg, 1)
    g.wait_ge(S.cv, 4)
    g.affine_select(T.tri[:], T.ones[:], [[1, 16], [0, 16]], AluOpType.is_gt, 0.0, 0, -1).then_inc(S.cg, 1)
    g.affine_select(T.tri2[:], T.ones[:, 0:16], [[1, 16]], AluOpType.is_ge, 0.0, 0, -1).then_inc(S.cg, 1)

    g.vector.wait_ge(S.ci, 16)
    g.vector.tensor_scalar(T.cf[:], T.cin[:, 0:1], float(-CAP), None, AluOpType.add).then_inc(S.vs, 1)
    g.vector.wait_ge(S.vs, 1)
    g.vector.wait_ge(S.cv, 4)
    g.vector.tensor_scalar(T.lhs[:], T.ones[:, 0:128], T.cf[:, 0:1], None, AluOpType.mult).then_inc(S.lh, 1)
    t = g.tensor
    t.wait_ge(S.cv, 4)
    t.wait_ge(S.cg, 4)
    for ps in (T.ps1, T.ps2):
        t.matmul(ps[:, 0:256], T.six[0:1, :], T.cidx[0:1, :], True, False)
        t.matmul(ps[:, 0:256], T.qrow[0:1, :], T.ones[0:1, :], False, False)
    t.wait_ge(S.lh, 1)
    t.matmul(T.ps1[:, 0:256], T.lhs[:], T.tri[:], False, True).then_inc(S.mm1, 1)
    g.vector.wait_ge(S.mm1, 1)
    g.vector.tensor_copy(T.off[:], T.ps1[:, 0:256]).then_inc(S.ofs, 1)

    def v_gather(out, win, lst, sem):
        g.vector.tensor_copy(out, win.indirect(lst)).then_inc(sem, 1)

    def s_gather(out, win, lst, sem):
        g.scalar.activation(out, win.indirect(lst), ActivationFunctionType.Identity, bias=T.nz[:, 0:1],
                            scale=1.0).then_inc(sem, 1)

    def pack(gather, out, ranks, sem, soon):
        gather(out, T.xs[:, :HALF] if soon else T.xs[:], T.off[:, 16 * ranks[0]:16 * (ranks[-1] + 1)], sem)

    plan = [("D0", diag[:2], piece(T.snd, diag[0], 1), piece(T.snd, diag[1], 1)),
            ("D1", diag[2:], piece(T.snd, diag[2], 1), piece(T.snd, diag[3], 1)),
            ("N", near, piece(T.hsn, 0, 2), piece(T.hsn, 2, 2)),
            ("H", cabled[2:], piece(T.hsn, 4, 1), piece(T.hsn, 5, 1)),
            ("C", cabled[:2], piece(T.snd, cabled[0], 1), piece(T.snd, cabled[1], 1))]
    soon = [e for e in plan if early(e[1])]
    late = [e for e in plan if not early(e[1])]
    for q in (g.vector, g.scalar):
        q.wait_ge(S.ofs, 1)
        q.wait_ge(S.xl0, 16)
    g.scalar.wait_ge(S.cv, 4)
    for entries, first in ((soon, True), (late, False)):
        if not first:
            g.vector.wait_ge(S.xl1, 16)
            g.scalar.wait_ge(S.xl1, 16)
        for name, ranks, v_out, s_out in entries:
            n = len(ranks) // 2
            pack(v_gather, v_out, ranks[:n], S["g" + name], first)
            pack(s_gather, s_out, ranks[n:], S["g" + name], first)
    for k, r in enumerate(groups[a]):
        pack(v_gather if k < 2 else s_gather, (T.land if r == rank else T.snd)[:, blocks([r])], [r], S.gO, early([r]))

    n_sent = [0]

    def fused(transfers, engines):
        g.remote_dma_fused(transfers, local_sem=S.sent)
        n_sent[0] += engines

    def deliver(ranks, masks):
        fused([move(T.cores[r], m, S.arr, T.snd[:, blocks([r])], T.land[:, blocks([rank])]) for r, m in zip(ranks, masks)],
              sum(len(bits(m)) for r, m in zip(ranks, masks)))

    def to_helper(sem, k, n):
        rid, pid = topo.addr(my_helper, core)
        g.remote_dma(piece(T.hdb, k, n), piece(T.hsn, k, n), sem, S.sent, pid, rid, here)
        n_sent[0] += len(bits(here))

    def to_porters(ks):
        fused([move(my_porters[k], m, S.hd, T.snd[:, blocks([diag[k]])], T.dd[:]) for k, m in zip(ks, f4)], 8)

    slot = T.call[rank]
    f4 = parts(far, 4)
    g.wait_ge(S.cl, 32)
    fused([move(my_helper, f4[0], S.hl, slot, slot),
           RemoteDMATransfer(dst_ids=[dst(p) for p in my_porters], dma_engine_mask=f4[1], remote_sem=S.hc, srcs=[slot],
                             dsts=[slot] * len(my_porters))], 8)
    for entry in soon + late:
        name = entry[0]
        g.wait_ge(S["g" + name], 2)
        if name == "D0":
            to_porters((0, 1))
        elif name == "D1":
            to_porters((2, 3))
        elif name == "N":
            to_helper(S.hn, 0, 4)
        elif name == "H":
            to_helper(S.hs, 4, 2)
        else:
            deliver(cabled[:2], f4)
    g.wait_ge(S.gO, 4)
    deliver(mates_here[:2], parts(here, 4))
    deliver(mates_here[2:], [here])

    g.sync.wait_ge(S.cl, 32)
    g.sync.wait_ge(S.carr, 4 * 3 + 4 * 4 + 8 * 4 + 8 * 4)
    g.sync.dma_start(T.ctab[:], T.call[:, 0:16, :]).then_inc(S.ct, 16)
    v, A = g.vector, AluOpType
    got = T.ctab[:, 2 * rank:2 * rank + 1]
    v.wait_ge(S.ct, 16)
    v.tensor_copy(T.cb[:], got).then_inc(S.cbs, 1)
    v.tensor_scalar(T.dr[:], got, -1.0, float(CAP), A.mult, A.add).then_inc(S.vq, 1)
    t.wait_ge(S.cbs, 1)
    t.matmul(T.ps3[0:16, 0:1], T.tri2[:], T.cb[:], True, True).then_inc(S.mb, 1)
    B = T.ps3[0:16, 0:1]
    v.wait_ge(S.mb, 1)
    v.tensor_copy(T.bi[:], B).then_inc(S.vq, 1)
    v.tensor_scalar(T.t1[:], B, -15.0, 1.0 / 16, A.add, A.mult).then_inc(S.vq, 1)
    v.tensor_scalar(T.t2[:], B, 1.0, 1.0 / 16, A.add, A.mult).then_inc(S.vq, 1)
    v.wait_ge(S.vq, 4)
    v.tensor_scalar(T.bl[:], T.bi[:], 15, None, A.bitwise_and).then_inc(S.vq, 1)
    v.wait_ge(S.cg, 4)
    v.tensor_scalar(T.rg1[:], T.cidx[:], T.t1[:, 0:1], None, A.is_ge).then_inc(S.rl, 1)
    v.wait_ge(S.vq, 5)
    v.tensor_copy(T.blf[:], T.bl[:]).then_inc(S.vq, 1)
    v.tensor_scalar(T.rg2[:], T.cidx[:], T.t2[:, 0:1], None, A.is_ge).then_inc(S.rl, 1)
    v.wait_ge(S.vq, 6)
    v.tensor_scalar(T.lg1[:], T.qrow[:], T.blf[:, 0:1], T.dr[:, 0:1], A.is_ge, A.mult).then_inc(S.rl, 1)
    v.tensor_scalar(T.lg2[:], T.qrow[:], T.blf[:, 0:1], T.dr[:, 0:1], A.is_lt, A.mult).then_inc(S.rl, 1)
    t.wait_ge(S.rl, 4)
    t.matmul(T.ps2[:, 0:256], T.lg1[:], T.rg1[:], False, False)
    t.matmul(T.ps2[:, 0:256], T.lg2[:], T.rg2[:], False, True).then_inc(S.mm2, 1)
    v.wait_ge(S.mm2, 1)
    v.tensor_scalar(T.offr[:], T.ps2[:, 0:256], float(W), None, A.min).then_inc(S.ofr, 1)

    arrivals = 2 * 4 + 4 * 4 + 8 * 4
    for r in mates_here:
        arrivals += 8 if [q for q in groups[a] if q != r][-1] == rank else 4
    for q in (g.vector, g.scalar):
        q.wait_ge(S.ofr, 1)
        q.wait_ge(S.gO, 4)
        q.wait_ge(S.arr, arrivals)
    p = 0
    for k, w in enumerate(PIECES):
        ready = S["y%d" % k]
        (v_gather if k % 2 == 0 else s_gather)(T.outb[:, p:p + w], T.land[:], T.offr[:, p // 16:(p + w) // 16], ready)
        g.sync.wait_ge(ready, 1)
        g.sync.dma_start(T.y[:, p:p + w], T.outb[:, p:p + w]).then_inc(S.stored, 16)
        p += w
    g.sync.wait_ge(S.stored, 16 * len(PIECES))
    g.wait_ge(S.sent, n_sent[0])
